import numpy as np
import ml_dtypes


def mxq(x, axis, fmt="e4m3"):
    dtype, down = {"e4m3": (ml_dtypes.float8_e4m3fn, 7), "e5m2": (ml_dtypes.float8_e5m2, 14)}[fmt]
    v = np.moveaxis(np.asarray(x, np.float32).astype(ml_dtypes.bfloat16).astype(np.float64), axis, -1)
    blocks = v.reshape(v.shape[:-1] + (-1, 32))
    amax = np.abs(blocks).max(-1, keepdims=True)
    byte = np.maximum(np.where(amax > 0, np.frexp(amax)[1] - 1 + 127, 0) - down, 1)
    scale = np.exp2(byte - 127.0)
    codes = (blocks / scale).astype(np.float32).astype(dtype).astype(np.float64)
    return np.moveaxis((codes * scale).reshape(v.shape), -1, axis)


WIDE = False


def mx_kscale(k):
    if not WIDE:
        return np.ones(k)
    levels = np.array([30, -30])
    if k % 512:
        return np.exp2(np.random.permutation(np.resize(levels, k // 32))).repeat(32)
    a = np.empty((k // 512, 16))
    for p in range(k // 512):
        a[p, :8] = np.random.permutation(np.resize(levels, 8))
        for g in range(8):
            far = levels[np.abs(levels - a[p, g]) >= 10]
            a[p, g + 8] = far[np.random.randint(len(far))]
    return np.exp2(a.ravel()).repeat(32)


def f64(x):
    return np.asarray(x).astype(np.float64)


def striped(idx):
    return np.tile(np.asarray(idx).reshape(-1, 16).T, (8, 1)).astype(np.uint16)


def unstriped(offs):
    return offs[:16].T.reshape(-1).astype(np.int64)


K, J, N, T, V, C, Q = 256, 1024, 256, 2048, 2048, 128, 1024


def setup_inputs():
    n = np.random.standard_normal
    idx = np.random.permutation(T)[:J]
    idx2 = np.random.permutation(V)[:J]
    idx3 = np.random.permutation(Q)[:N]
    fj = mx_kscale(J)
    return {
        "xf": (n((K, T))).astype(np.float32),
        "ra": (np.random.uniform(0.5, 1.5, (1, J)) * fj).astype(np.float32),
        "ow": (n((K, J)) * 0.7).astype(np.float32),
        "gt": (n((N, V)) * np.exp(0.5 * n((1, V)))).astype(np.float32),
        "rb": (np.random.uniform(0.5, 1.5, (1, J)) / fj).astype(np.float32),
        "old": (0.5 * n((K, Q))).astype(np.float32),
        "offs": striped(idx),
        "offs2": striped(idx2),
        "offs3": striped(idx3),
    }


def reference(xf, ra, ow, gt, rb, old, offs, offs2, offs3):
    idx = unstriped(offs)
    idx2 = unstriped(offs2)
    idx3 = unstriped(offs3)
    us = (f64(xf)[:, idx] - f64(ow)) * f64(ra)
    uj = us.T
    gg = f64(gt)[:, idx2]
    c1 = gg.reshape(N, C, J // C).mean(axis=2)
    c2 = np.repeat(c1, J // C, axis=1)
    gs = (gg - c2) * f64(rb)
    gj = gs.T
    ujq = mxq(uj, 0, "e5m2")
    gjq = mxq(gj, 0, "e5m2")
    w = ujq.T @ gjq
    wp = np.zeros((K, Q))
    wp[:, idx3] = w
    y = 0.04 * wp + f64(old)
    return y

@@ -1,0 +1,176 @@
+from contextlib import ExitStack
+
+import concourse.mybir as mybir
+from concourse.masks import make_identity
+
+K, J, N, T, Q = 256, 1024, 256, 2048, 1024
+FLOPS = 2 * K * N * J
+
+F32 = mybir.dt.float32
+BF16 = mybir.dt.bfloat16
+U32 = mybir.dt.uint32
+U16 = mybir.dt.uint16
+U8 = mybir.dt.uint8
+E5M2X4 = mybir.dt.float8_e5m2_x4
+ALU = mybir.AluOpType
+COPY = mybir.ActivationFunctionType.Copy
+
+P = 128
+PACK = 4
+J_PASS = P * PACK
+PASSES = J // J_PASS
+SET = 8
+LIST_COLS = J_PASS // 16
+
+
+def tile_list_moment_offset_centred_placed_kernel(tc, xf, ra, ow, gt, rb, old, offs, offs2, offs3, out):
+    nc = tc.nc
+    with ExitStack() as ctx:
+        keep = ctx.enter_context(tc.tile_pool(name="keep", bufs=1))
+        turn_psum = ctx.enter_context(tc.psum_pool(name="turn_psum", bufs=6))
+        acc_psum = ctx.enter_context(tc.psum_pool(name="acc_psum", bufs=2))
+
+        def rows(i):
+            return slice(i * P, (i + 1) * P)
+
+        def slots(a):
+            return slice(a * J_PASS, (a + 1) * J_PASS)
+
+        x_list = keep.tile([P, J // 16], U16, name="x_list")
+        g_list = keep.tile([P, J // 16], U16, name="g_list")
+        w_list = keep.tile([P, N // 16], U16, name="w_list")
+        g_tab = [keep.tile([P, T], F32, name="g_tab%d" % i) for i in range(2)]
+        x_tab = [keep.tile([P, T], F32, name="x_tab%d" % i) for i in range(2)]
+        own0 = keep.tile([P, J], F32, name="own0")
+        own1 = [keep.tile([P, J_PASS], F32, name="own1_%d" % a) for a in range(PASSES)]
+        old_sb = [keep.tile([P, Q], F32, name="old%d" % i) for i in range(2)]
+        ra_sb = keep.tile([P, PASSES, PACK], F32, name="ra_sb")
+        rb_sb = keep.tile([P, PASSES, PACK], F32, name="rb_sb")
+
+        nc.sync.dma_start(g_list[:], offs2)
+        nc.sync.dma_start(g_tab[0][:], gt[rows(0), :])
+        nc.scalar.dma_start(rb_sb[:], rb.rearrange("o (a p t) -> (o p) a t", a=PASSES, t=PACK))
+        nc.scalar.dma_start(ra_sb[:], ra.rearrange("o (a p t) -> (o p) a t", a=PASSES, t=PACK))
+        nc.sync.dma_start(g_tab[1][:], gt[rows(1), :])
+        nc.sync.dma_start(x_list[:], offs)
+        nc.sync.dma_start(x_tab[0][:], xf[rows(0), :])
+        nc.sync.dma_start(own0[:], ow[rows(0), :])
+        nc.sync.dma_start(x_tab[1][:], xf[rows(1), :])
+        for a in range(PASSES):
+            nc.sync.dma_start(own1[a][:], ow[rows(1), slots(a)])
+        nc.sync.dma_start(w_list[:], offs3)
+        for i in range(2):
+            nc.sync.dma_start(old_sb[i][:], old[rows(i), :])
+
+        ident = keep.tile([P, P], F32, name="ident")
+        make_identity(nc, ident[:])
+        page = [keep.tile([P, Q], F32, name="page%d" % i) for i in range(2)]
+        for i in range(2):
+            nc.gpsimd.memset(page[i][:], 0.0)
+
+        def gather(tab, lst, a, on_vector, name):
+            picked = keep.tile([P, J_PASS], F32, name=name)
+            src = tab[:].indirect(lst[:, a * LIST_COLS:(a + 1) * LIST_COLS])
+            if on_vector:
+                nc.vector.tensor_copy(picked[:], src)
+            else:
+                nc.scalar.activation(picked[:], src, COPY)
+            return picked
+
+        def centre(picked, name):
+            sums = keep.tile([P, J_PASS // SET], F32, name=name + "_sums")
+            nc.vector.tensor_reduce(sums[:], picked[:].rearrange("p (c r) -> p c r", r=SET), mybir.AxisListType.X, ALU.add)
+            dealt = keep.tile([P, PACK, P], F32, name=name + "_dealt")
+            nc.vector.scalar_tensor_tensor(
+                out=dealt[:].rearrange("p t q -> p q t"),
+                in0=sums[:].unsqueeze(2).to_broadcast([P, J_PASS // SET, SET]),
+                scalar=-1.0 / SET,
+                in1=picked[:].rearrange("p (c r) -> p c r", r=SET),
+                op0=ALU.mult,
+                op1=ALU.add,
+            )
+            return dealt
+
+        def offset(picked, own, name):
+            dealt = keep.tile([P, PACK, P], F32, name=name + "_dealt")
+            nc.vector.tensor_tensor(
+                out=dealt[:].rearrange("p t q -> p q t"),
+                in0=picked[:].rearrange("p (q t) -> p q t", t=PACK),
+                in1=own.rearrange("p (q t) -> p q t", t=PACK),
+                op=ALU.subtract,
+            )
+            return dealt
+
+        def turn(dealt):
+            bank = turn_psum.tile([P, PACK, P], F32, name="bank")
+            for t in range(PACK):
+                nc.tensor.transpose(bank[:, t, :], dealt[:, t, :], ident[:])
+            return bank
+
+        def weigh(bank, weight, grouped):
+            nc.vector.tensor_tensor(
+                out=grouped,
+                in0=bank[:].rearrange("p t c -> p c t"),
+                in1=weight.unsqueeze(1).to_broadcast([P, P, PACK]),
+                op=ALU.mult,
+            )
+
+        def quantise(grouped, width, name):
+            codes = keep.tile([P, width], U32, name=name + "_codes", align_bytes=64)
+            scales = keep.tile([P, width], U8, name=name + "_scales", align_bytes=64)
+            nc.vector.quantize_mx(out=codes[:].bitcast(E5M2X4), scales=scales[:], in_=grouped[:].rearrange("p c t -> p (c t)"))
+            return codes, scales
+
+        def product(u_q, g_q):
+            acc = acc_psum.tile([P, N], F32, name="acc")
+            for a in range(PASSES):
+                nc.tensor.matmul_mx(
+                    out=acc[:],
+                    lhsT=u_q[a][0][:].bitcast(E5M2X4),
+                    lhsT_scale=u_q[a][1][:],
+                    rhs=g_q[a][0][:].bitcast(E5M2X4),
+                    rhs_scale=g_q[a][1][:],
+                    start=(a == 0),
+                    stop=(a == PASSES - 1),
+                )
+            return acc
+
+        def place(acc, i):
+            w_sb = keep.tile([P, N], F32, name="w_sb%d" % i)
+            nc.scalar.copy(w_sb[:], acc[:])
+            nc.scalar.activation(page[i][:].indirect(w_list[:]), w_sb[:], COPY)
+
+        def finish(i):
+            for h in range(2):
+                cols = slice(h * Q // 2, (h + 1) * Q // 2)
+                res = keep.tile([P, Q // 2], F32, name="res%d_%d" % (i, h))
+                nc.vector.scalar_tensor_tensor(
+                    out=res[:], in0=page[i][:, cols], scalar=0.04, in1=old_sb[i][:, cols], op0=ALU.mult, op1=ALU.add
+                )
+                nc.sync.dma_start(out[rows(i), cols], res[:])
+
+        g_grouped = [keep.tile([P, N, PACK], BF16, name="g_grouped%d" % a, align_bytes=64) for a in range(PASSES)]
+        u_grouped = [
+            [keep.tile([P, P, PACK], BF16, name="u_grouped%d_%d" % (i, a), align_bytes=64) for a in range(PASSES)]
+            for i in range(2)
+        ]
+
+        gp = [[gather(g_tab[i], g_list, a, i == 0 and a == 1, "gp%d_%d" % (i, a)) for a in range(PASSES)] for i in range(2)]
+        xp = [[gather(x_tab[i], x_list, a, False, "xp%d_%d" % (i, a)) for a in range(PASSES)] for i in range(2)]
+
+        for i in range(2):
+            banks = [turn(centre(gp[i][a], "g%d_%d" % (i, a))) for a in range(PASSES)]
+            for a in range(PASSES):
+                weigh(banks[a], rb_sb[:, a, :], g_grouped[a][:, rows(i), :])
+        own = [[own0[:, slots(a)] for a in range(PASSES)], [own1[a][:] for a in range(PASSES)]]
+        g_q = []
+        for i in range(2):
+            banks = [turn(offset(xp[i][a], own[i][a], "u%d_%d" % (i, a))) for a in range(PASSES)]
+            if i == 0:
+                g_q = [quantise(g_grouped[a], N, "g%d" % a) for a in range(PASSES)]
+            for a in range(PASSES):
+                weigh(banks[a], ra_sb[:, a, :], u_grouped[i][a][:])
+            u_q = [quantise(u_grouped[i][a], P, "u%d_%d" % (i, a)) for a in range(PASSES)]
+            place(product(u_q, g_q), i)
+        for i in range(2):
+            finish(i)

@@ -1,7 +1,6 @@
 from contextlib import ExitStack
 
 import concourse.mybir as mybir
-from concourse.masks import make_identity
 
 K, J, N, T, Q = 256, 1024, 256, 2048, 1024
 FLOPS = 2 * K * N * J
@@ -47,13 +46,30 @@ def tile_list_moment_offset_centred_placed_kernel(tc, xf, ra, ow, gt, rb, old, o
         ra_sb = keep.tile([P, PASSES, PACK], F32, name="ra_sb")
         rb_sb = keep.tile([P, PASSES, PACK], F32, name="rb_sb")
 
+        ones = keep.tile([P, P], F32, name="ones")
+        nc.vector.memset(ones[:], 1.0)
+        ramp = keep.tile([P, P], F32, name="ramp", align_bytes=64)
+        nc.vector.tensor_tensor_scan(ramp[:], ones[:], ones[:], -1.0, ALU.mult, ALU.add)
+        turned = keep.tile([P, P], F32, name="turned", align_bytes=64)
+        nc.vector.transpose(turned[:], ramp[:])
+        ident = keep.tile([P, P], F32, name="ident")
+        for quad in range(4):
+            part = slice(32 * quad, 32 * quad + 32)
+            nc.vector.tensor_scalar(ident[part, :], ramp[part, :], turned[part, 32 * quad:32 * quad + 1], None, ALU.is_equal)
+
+        def load_table(tab, src):
+            nc.sync.dma_start(tab[:, 0:T // 2], src[:, 0:T // 2])
+            nc.scalar.dma_start(tab[:, T // 2:T], src[:, T // 2:T])
+
         nc.sync.dma_start(g_list[:], offs2)
-        nc.sync.dma_start(g_tab[0][:], gt[rows(0), :])
-        nc.scalar.dma_start(rb_sb[:], rb.rearrange("o (a p t) -> (o p) a t", a=PASSES, t=PACK))
-        nc.scalar.dma_start(ra_sb[:], ra.rearrange("o (a p t) -> (o p) a t", a=PASSES, t=PACK))
-        nc.sync.dma_start(g_tab[1][:], gt[rows(1), :])
+        load_table(g_tab[0], gt[rows(0), :])
+        warm = keep.tile([P, 1], F32, name="warm")
+        nc.scalar.activation(warm[:], ones[:, 0:1], COPY)
+        load_table(g_tab[1], gt[rows(1), :])
         nc.sync.dma_start(x_list[:], offs)
-        nc.sync.dma_start(x_tab[0][:], xf[rows(0), :])
+        nc.scalar.dma_start(rb_sb[:], rb.rearrange("o (a p t) -> (o p) a t", a=PASSES, t=PACK))
+        load_table(x_tab[0], xf[rows(0), :])
+        nc.scalar.dma_start(ra_sb[:], ra.rearrange("o (a p t) -> (o p) a t", a=PASSES, t=PACK))
         nc.sync.dma_start(own0[:], ow[rows(0), :])
         nc.sync.dma_start(x_tab[1][:], xf[rows(1), :])
         for a in range(PASSES):
@@ -62,20 +78,35 @@ def tile_list_moment_offset_centred_placed_kernel(tc, xf, ra, ow, gt, rb, old, o
         for i in range(2):
             nc.sync.dma_start(old_sb[i][:], old[rows(i), :])
 
-        ident = keep.tile([P, P], F32, name="ident")
-        make_identity(nc, ident[:])
         page = [keep.tile([P, Q], F32, name="page%d" % i) for i in range(2)]
         for i in range(2):
-            nc.gpsimd.memset(page[i][:], 0.0)
+            nc.vector.memset(page[i][:], 0.0)
 
-        def gather(tab, lst, a, on_vector, name):
-            picked = keep.tile([P, J_PASS], F32, name=name)
-            src = tab[:].indirect(lst[:, a * LIST_COLS:(a + 1) * LIST_COLS])
-            if on_vector:
-                nc.vector.tensor_copy(picked[:], src)
-            else:
-                nc.scalar.activation(picked[:], src, COPY)
+        def gather(tab, lst, a, vector_cols, name):
+            picked = keep.tile([P, J_PASS], F32, name=name, tag=name)
+            c0 = a * LIST_COLS
+            if vector_cols > 0:
+                nc.vector.tensor_copy(picked[:, 0:16 * vector_cols], tab[:].indirect(lst[:, c0:c0 + vector_cols]))
+            if vector_cols < LIST_COLS:
+                nc.scalar.activation(picked[:, 16 * vector_cols:J_PASS], tab[:].indirect(lst[:, c0 + vector_cols:c0 + LIST_COLS]), COPY)
             return picked
+
+        def neg_mean(picked, name):
+            sums = keep.tile([P, J_PASS // SET], F32, name=name + "_sums")
+            nc.vector.tensor_reduce(sums[:], picked[:].rearrange("p (c r) -> p c r", r=SET), mybir.AxisListType.X, ALU.add)
+            twice = keep.tile([P, J_PASS // SET, 2], F32, name=name + "_twice")
+            nc.vector.tensor_scalar(twice[:], sums[:].unsqueeze(2).to_broadcast([P, J_PASS // SET, 2]), -1.0 / SET, 0.0, ALU.mult, ALU.add)
+            return twice
+
+        def turn_open(picked):
+            bank = turn_psum.tile([P, PACK, P], F32, name="bank")
+            for t in range(PACK):
+                nc.tensor.matmul(bank[:, t, :], picked[:, t:J_PASS:PACK], ident[:], start=(t == 0), stop=False, is_transpose=True)
+            return bank
+
+        def turn_close(bank, twice):
+            for t in range(PACK):
+                nc.tensor.matmul(bank[:, t, :], twice[:].rearrange("p c h -> p (c h)"), ident[:], start=False, stop=(t == PACK - 1), is_transpose=True)
 
         def centre(picked, name):
             sums = keep.tile([P, J_PASS // SET], F32, name=name + "_sums")
@@ -136,41 +167,82 @@ def tile_list_moment_offset_centred_placed_kernel(tc, xf, ra, ow, gt, rb, old, o
             return acc
 
         def place(acc, i):
-            w_sb = keep.tile([P, N], F32, name="w_sb%d" % i)
+            w_sb = keep.tile([P, N], F32, name="w_sb%d" % i, tag="xp1_0" if i == 0 else "w_sb1")
             nc.scalar.copy(w_sb[:], acc[:])
             nc.scalar.activation(page[i][:].indirect(w_list[:]), w_sb[:], COPY)
 
-        def finish(i):
-            for h in range(2):
-                cols = slice(h * Q // 2, (h + 1) * Q // 2)
-                res = keep.tile([P, Q // 2], F32, name="res%d_%d" % (i, h))
+        def finish(i, cuts):
+            for h in range(len(cuts) - 1):
+                cols = slice(cuts[h], cuts[h + 1])
+                res = keep.tile([P, cuts[h + 1] - cuts[h]], F32, name="res%d_%d" % (i, h), tag="last" if (i, h) == (0, 0) else "res%d_%d" % (i, h), align_bytes=64)
                 nc.vector.scalar_tensor_tensor(
                     out=res[:], in0=page[i][:, cols], scalar=0.04, in1=old_sb[i][:, cols], op0=ALU.mult, op1=ALU.add
                 )
                 nc.sync.dma_start(out[rows(i), cols], res[:])
 
-        g_grouped = [keep.tile([P, N, PACK], BF16, name="g_grouped%d" % a, align_bytes=64) for a in range(PASSES)]
-        u_grouped = [
-            [keep.tile([P, P, PACK], BF16, name="u_grouped%d_%d" % (i, a), align_bytes=64) for a in range(PASSES)]
+        g_grouped = [
+            [keep.tile([P, P, PACK], BF16, name="g_grouped%d_%d" % (i, a), align_bytes=64) for a in range(PASSES)]
             for i in range(2)
         ]
+        g_q = [
+            (keep.tile([P, N], U32, name="g_codes%d" % a, align_bytes=64), keep.tile([P, N], U8, name="g_scales%d" % a, align_bytes=64))
+            for a in range(PASSES)
+        ]
 
-        gp = [[gather(g_tab[i], g_list, a, i == 0 and a == 1, "gp%d_%d" % (i, a)) for a in range(PASSES)] for i in range(2)]
-        xp = [[gather(x_tab[i], x_list, a, False, "xp%d_%d" % (i, a)) for a in range(PASSES)] for i in range(2)]
-
-        for i in range(2):
-            banks = [turn(centre(gp[i][a], "g%d_%d" % (i, a))) for a in range(PASSES)]
-            for a in range(PASSES):
-                weigh(banks[a], rb_sb[:, a, :], g_grouped[a][:, rows(i), :])
+        def g_quantise(i, a):
+            nc.vector.quantize_mx(out=g_q[a][0][:, rows(i)].bitcast(E5M2X4), scales=g_q[a][1][:, rows(i)], in_=g_grouped[i][a][:].rearrange("p c t -> p (c t)"))
+        u_grouped = [
+            [keep.tile([P, P, PACK], BF16, name="u_grouped%d_%d" % (i, a), tag="last" if (i, a) == (1, 1) else "ug%d_%d" % (i, a), align_bytes=64) for a in range(PASSES)]
+            for i in range(2)
+        ]
         own = [[own0[:, slots(a)] for a in range(PASSES)], [own1[a][:] for a in range(PASSES)]]
-        g_q = []
-        for i in range(2):
-            banks = [turn(offset(xp[i][a], own[i][a], "u%d_%d" % (i, a))) for a in range(PASSES)]
-            if i == 0:
-                g_q = [quantise(g_grouped[a], N, "g%d" % a) for a in range(PASSES)]
-            for a in range(PASSES):
-                weigh(banks[a], ra_sb[:, a, :], u_grouped[i][a][:])
-            u_q = [quantise(u_grouped[i][a], P, "u%d_%d" % (i, a)) for a in range(PASSES)]
-            place(product(u_q, g_q), i)
-        for i in range(2):
-            finish(i)
+
+        gp = [[gather(g_tab[i], g_list, a, 16 if (i, a) == (0, 0) else 0, "gp%d_%d" % (i, a)) for a in range(PASSES)] for i in range(2)]
+        xp = [[gather(x_tab[i], x_list, a, 0, "xp%d_%d" % (i, a)) for a in range(PASSES)] for i in range(2)]
+
+        def g_turn(i, a):
+            twice = neg_mean(gp[i][a], "g%d_%d" % (i, a))
+            bank = turn_open(gp[i][a])
+            turn_close(bank, twice)
+            return bank
+
+        def g_weigh(bank, i, a):
+            weigh(bank, rb_sb[:, a, :], g_grouped[i][a][:])
+
+        def u_turn(i, a):
+            return turn(offset(xp[i][a], own[i][a], "u%d_%d" % (i, a)))
+
+        def u_weigh(bank, i, a):
+            weigh(bank, ra_sb[:, a, :], u_grouped[i][a][:])
+
+        def u_quantise(i, a):
+            return quantise(u_grouped[i][a], P, "u%d_%d" % (i, a))
+
+        b00 = g_turn(0, 0)
+        b01 = g_turn(0, 1)
+        b10 = g_turn(1, 0)
+        g_weigh(b00, 0, 0)
+        b11 = g_turn(1, 1)
+        g_weigh(b01, 0, 1)
+        g_quantise(0, 0)
+        c00 = u_turn(0, 0)
+        g_quantise(0, 1)
+        c01 = u_turn(0, 1)
+        g_weigh(b10, 1, 0)
+        g_weigh(b11, 1, 1)
+        g_quantise(1, 0)
+        u_weigh(c00, 0, 0)
+        g_quantise(1, 1)
+        u_weigh(c01, 0, 1)
+        q00 = u_quantise(0, 0)
+        c10 = u_turn(1, 0)
+        q01 = u_quantise(0, 1)
+        place(product([q00, q01], g_q), 0)
+        c11 = u_turn(1, 1)
+        u_weigh(c10, 1, 0)
+        q10 = u_quantise(1, 0)
+        u_weigh(c11, 1, 1)
+        q11 = u_quantise(1, 1)
+        place(product([q10, q11], g_q), 1)
+        finish(0, [0, 1024])
+        finish(1, [0, 256, 512, 768, 1024])

@@ -82,13 +82,13 @@ def tile_list_moment_offset_centred_placed_kernel(tc, xf, ra, ow, gt, rb, old, o
         for i in range(2):
             nc.vector.memset(page[i][:], 0.0)
 
-        def gather(tab, lst, a, vector_cols, name):
+        def gather(tab, lst, a, vector_cols, name, sign=1.0):
             picked = keep.tile([P, J_PASS], F32, name=name, tag=name)
             c0 = a * LIST_COLS
             if vector_cols > 0:
                 nc.vector.tensor_copy(picked[:, 0:16 * vector_cols], tab[:].indirect(lst[:, c0:c0 + vector_cols]))
             if vector_cols < LIST_COLS:
-                nc.scalar.activation(picked[:, 16 * vector_cols:J_PASS], tab[:].indirect(lst[:, c0 + vector_cols:c0 + LIST_COLS]), COPY)
+                nc.scalar.activation(picked[:, 16 * vector_cols:J_PASS], tab[:].indirect(lst[:, c0 + vector_cols:c0 + LIST_COLS]), COPY, scale=sign)
             return picked
 
         def neg_mean(picked, name):
@@ -138,6 +138,23 @@ def tile_list_moment_offset_centred_placed_kernel(tc, xf, ra, ow, gt, rb, old, o
                 nc.tensor.transpose(bank[:, t, :], dealt[:, t, :], ident[:])
             return bank
 
+        def turn_sum(first, second):
+            bank = turn_psum.tile([P, PACK, P], F32, name="bank")
+            for s, src in enumerate((first, second)):
+                for t in range(PACK):
+                    nc.tensor.matmul(bank[:, t, :], src[:, t:J_PASS:PACK], ident[:], start=(s == 0 and t == 0), stop=(s == 1 and t == PACK - 1), is_transpose=True)
+            return bank
+
+        def weigh_negated(bank, weight, grouped):
+            nc.vector.scalar_tensor_tensor(
+                out=grouped,
+                in0=bank[:].rearrange("p t c -> p c t"),
+                scalar=-1.0,
+                in1=weight.unsqueeze(1).to_broadcast([P, P, PACK]),
+                op0=ALU.mult,
+                op1=ALU.mult,
+            )
+
         def weigh(bank, weight, grouped):
             nc.vector.tensor_tensor(
                 out=grouped,
@@ -147,7 +164,7 @@ def tile_list_moment_offset_centred_placed_kernel(tc, xf, ra, ow, gt, rb, old, o
             )
 
         def quantise(grouped, width, name):
-            codes = keep.tile([P, width], U32, name=name + "_codes", align_bytes=64)
+            codes = keep.tile([P, width], U32, name=name + "_codes", tag="last" if name == "u1_1" else name + "_codes", align_bytes=64)
             scales = keep.tile([P, width], U8, name=name + "_scales", align_bytes=64)
             nc.vector.quantize_mx(out=codes[:].bitcast(E5M2X4), scales=scales[:], in_=grouped[:].rearrange("p c t -> p (c t)"))
             return codes, scales
@@ -168,7 +185,10 @@ def tile_list_moment_offset_centred_placed_kernel(tc, xf, ra, ow, gt, rb, old, o
 
         def place(acc, i):
             w_sb = keep.tile([P, N], F32, name="w_sb%d" % i, tag="xp1_0" if i == 0 else "w_sb1")
-            nc.scalar.copy(w_sb[:], acc[:])
+            if i == 0:
+                nc.scalar.copy(w_sb[:], acc[:])
+            else:
+                nc.vector.tensor_copy(w_sb[:], acc[:])
             nc.scalar.activation(page[i][:].indirect(w_list[:]), w_sb[:], COPY)
 
         def finish(i, cuts):
@@ -192,13 +212,13 @@ def tile_list_moment_offset_centred_placed_kernel(tc, xf, ra, ow, gt, rb, old, o
         def g_quantise(i, a):
             nc.vector.quantize_mx(out=g_q[a][0][:, rows(i)].bitcast(E5M2X4), scales=g_q[a][1][:, rows(i)], in_=g_grouped[i][a][:].rearrange("p c t -> p (c t)"))
         u_grouped = [
-            [keep.tile([P, P, PACK], BF16, name="u_grouped%d_%d" % (i, a), tag="last" if (i, a) == (1, 1) else "ug%d_%d" % (i, a), align_bytes=64) for a in range(PASSES)]
+            [keep.tile([P, P, PACK], BF16, name="u_grouped%d_%d" % (i, a), align_bytes=64) for a in range(PASSES)]
             for i in range(2)
         ]
         own = [[own0[:, slots(a)] for a in range(PASSES)], [own1[a][:] for a in range(PASSES)]]
 
         gp = [[gather(g_tab[i], g_list, a, 16 if (i, a) == (0, 0) else 0, "gp%d_%d" % (i, a)) for a in range(PASSES)] for i in range(2)]
-        xp = [[gather(x_tab[i], x_list, a, 0, "xp%d_%d" % (i, a)) for a in range(PASSES)] for i in range(2)]
+        xp = [[gather(x_tab[i], x_list, a, 0, "xp%d_%d" % (i, a), -1.0 if (i, a) == (1, 0) else 1.0) for a in range(PASSES)] for i in range(2)]
 
         def g_turn(i, a):
             twice = neg_mean(gp[i][a], "g%d_%d" % (i, a))
@@ -235,11 +255,11 @@ def tile_list_moment_offset_centred_placed_kernel(tc, xf, ra, ow, gt, rb, old, o
         g_quantise(1, 1)
         u_weigh(c01, 0, 1)
         q00 = u_quantise(0, 0)
-        c10 = u_turn(1, 0)
+        c10 = turn_sum(own[1][0], xp[1][0][:])
         q01 = u_quantise(0, 1)
         place(product([q00, q01], g_q), 0)
         c11 = u_turn(1, 1)
-        u_weigh(c10, 1, 0)
+        weigh_negated(c10, ra_sb[:, 0, :], u_grouped[1][0][:])
         q10 = u_quantise(1, 0)
         u_weigh(c11, 1, 1)
         q11 = u_quantise(1, 1)

@@ -43,8 +43,8 @@ def tile_list_moment_offset_centred_placed_kernel(tc, xf, ra, ow, gt, rb, old, o
         own0 = keep.tile([P, J], F32, name="own0")
         own1 = [keep.tile([P, J_PASS], F32, name="own1_%d" % a) for a in range(PASSES)]
         old_sb = [keep.tile([P, Q], F32, name="old%d" % i) for i in range(2)]
-        ra_sb = keep.tile([P, PASSES, PACK], F32, name="ra_sb")
-        rb_sb = keep.tile([P, PASSES, PACK], F32, name="rb_sb")
+        ra_sb = keep.tile([P, PASSES, 2 * PACK], F32, name="ra_sb")
+        rb_sb = keep.tile([P, PASSES, 2 * PACK], F32, name="rb_sb")
 
         ones = keep.tile([P, P], F32, name="ones")
         nc.vector.memset(ones[:], 1.0)
@@ -67,9 +67,9 @@ def tile_list_moment_offset_centred_placed_kernel(tc, xf, ra, ow, gt, rb, old, o
         nc.scalar.activation(warm[:], ones[:, 0:1], COPY)
         load_table(g_tab[1], gt[rows(1), :])
         nc.sync.dma_start(x_list[:], offs)
-        nc.scalar.dma_start(rb_sb[:], rb.rearrange("o (a p t) -> (o p) a t", a=PASSES, t=PACK))
+        nc.scalar.dma_start(rb_sb[:, :, 0:PACK], rb.rearrange("o (a p t) -> (o p) a t", a=PASSES, t=PACK))
         load_table(x_tab[0], xf[rows(0), :])
-        nc.scalar.dma_start(ra_sb[:], ra.rearrange("o (a p t) -> (o p) a t", a=PASSES, t=PACK))
+        nc.scalar.dma_start(ra_sb[:, :, 0:PACK], ra.rearrange("o (a p t) -> (o p) a t", a=PASSES, t=PACK))
         nc.sync.dma_start(own0[:], ow[rows(0), :])
         nc.sync.dma_start(x_tab[1][:], xf[rows(1), :])
         for a in range(PASSES):
@@ -227,13 +227,13 @@ def tile_list_moment_offset_centred_placed_kernel(tc, xf, ra, ow, gt, rb, old, o
             return bank
 
         def g_weigh(bank, i, a):
-            weigh(bank, rb_sb[:, a, :], g_grouped[i][a][:])
+            weigh(bank, rb_sb[:, a, 0:PACK], g_grouped[i][a][:])
 
         def u_turn(i, a):
             return turn(offset(xp[i][a], own[i][a], "u%d_%d" % (i, a)))
 
         def u_weigh(bank, i, a):
-            weigh(bank, ra_sb[:, a, :], u_grouped[i][a][:])
+            weigh(bank, ra_sb[:, a, 0:PACK], u_grouped[i][a][:])
 
         def u_quantise(i, a):
             return quantise(u_grouped[i][a], P, "u%d_%d" % (i, a))
@@ -259,7 +259,7 @@ def tile_list_moment_offset_centred_placed_kernel(tc, xf, ra, ow, gt, rb, old, o
         q01 = u_quantise(0, 1)
         place(product([q00, q01], g_q), 0)
         c11 = u_turn(1, 1)
-        weigh_negated(c10, ra_sb[:, 0, :], u_grouped[1][0][:])
+        weigh_negated(c10, ra_sb[:, 0, 0:PACK], u_grouped[1][0][:])
         q10 = u_quantise(1, 0)
         u_weigh(c11, 1, 1)
         q11 = u_quantise(1, 1)

from contextlib import ExitStack

import concourse.mybir as mybir

K, J, N, T, Q = 256, 1024, 256, 2048, 1024
FLOPS = 2 * K * N * J

F32 = mybir.dt.float32
BF16 = mybir.dt.bfloat16
U32 = mybir.dt.uint32
U16 = mybir.dt.uint16
U8 = mybir.dt.uint8
E5M2X4 = mybir.dt.float8_e5m2_x4
ALU = mybir.AluOpType
COPY = mybir.ActivationFunctionType.Copy

P = 128
PACK = 4
J_PASS = P * PACK
PASSES = J // J_PASS
SET = 8
LIST_COLS = J_PASS // 16


def tile_list_moment_offset_centred_placed_kernel(tc, xf, ra, ow, gt, rb, old, offs, offs2, offs3, out):
    nc = tc.nc
    with ExitStack() as ctx:
        keep = ctx.enter_context(tc.tile_pool(name="keep", bufs=1))
        turn_psum = ctx.enter_context(tc.psum_pool(name="turn_psum", bufs=6))
        acc_psum = ctx.enter_context(tc.psum_pool(name="acc_psum", bufs=2))

        def rows(i):
            return slice(i * P, (i + 1) * P)

        def slots(a):
            return slice(a * J_PASS, (a + 1) * J_PASS)

        x_list = keep.tile([P, J // 16], U16, name="x_list")
        g_list = keep.tile([P, J // 16], U16, name="g_list")
        w_list = keep.tile([P, N // 16], U16, name="w_list")
        g_tab = [keep.tile([P, T], F32, name="g_tab%d" % i) for i in range(2)]
        x_tab = [keep.tile([P, T], F32, name="x_tab%d" % i) for i in range(2)]
        own0 = keep.tile([P, J], F32, name="own0")
        own1 = [keep.tile([P, J_PASS], F32, name="own1_%d" % a) for a in range(PASSES)]
        old_sb = [keep.tile([P, Q], F32, name="old%d" % i) for i in range(2)]
        ra_sb = keep.tile([P, PASSES, 2 * PACK], F32, name="ra_sb")
        rb_sb = keep.tile([P, PASSES, 2 * PACK], F32, name="rb_sb")

        ones = keep.tile([P, P], F32, name="ones")
        nc.vector.memset(ones[:], 1.0)
        ramp = keep.tile([P, P], F32, name="ramp", align_bytes=64)
        nc.vector.tensor_tensor_scan(ramp[:], ones[:], ones[:], -1.0, ALU.mult, ALU.add)
        turned = keep.tile([P, P], F32, name="turned", align_bytes=64)
        nc.vector.transpose(turned[:], ramp[:])
        ident = keep.tile([P, P], F32, name="ident")
        for quad in range(4):
            part = slice(32 * quad, 32 * quad + 32)
            nc.vector.tensor_scalar(ident[part, :], ramp[part, :], turned[part, 32 * quad:32 * quad + 1], None, ALU.is_equal)

        def load_table(tab, src):
            nc.sync.dma_start(tab[:, 0:T // 2], src[:, 0:T // 2])
            nc.scalar.dma_start(tab[:, T // 2:T], src[:, T // 2:T])

        nc.sync.dma_start(g_list[:], offs2)
        load_table(g_tab[0], gt[rows(0), :])
        warm = keep.tile([P, 1], F32, name="warm")
        nc.scalar.activation(warm[:], ones[:, 0:1], COPY)
        load_table(g_tab[1], gt[rows(1), :])
        nc.sync.dma_start(x_list[:], offs)
        nc.scalar.dma_start(rb_sb[:, :, 0:PACK], rb.rearrange("o (a p t) -> (o p) a t", a=PASSES, t=PACK))
        load_table(x_tab[0], xf[rows(0), :])
        nc.scalar.dma_start(ra_sb[:, :, 0:PACK], ra.rearrange("o (a p t) -> (o p) a t", a=PASSES, t=PACK))
        nc.sync.dma_start(own0[:], ow[rows(0), :])
        nc.sync.dma_start(x_tab[1][:], xf[rows(1), :])
        for a in range(PASSES):
            nc.sync.dma_start(own1[a][:], ow[rows(1), slots(a)])
        nc.sync.dma_start(w_list[:], offs3)
        for i in range(2):
            nc.sync.dma_start(old_sb[i][:], old[rows(i), :])

        page = [keep.tile([P, Q], F32, name="page%d" % i) for i in range(2)]
        for i in range(2):
            nc.vector.memset(page[i][:], 0.0)

        def gather(tab, lst, a, vector_cols, name, sign=1.0):
            picked = keep.tile([P, J_PASS], F32, name=name, tag=name)
            c0 = a * LIST_COLS
            if vector_cols > 0:
                nc.vector.tensor_copy(picked[:, 0:16 * vector_cols], tab[:].indirect(lst[:, c0:c0 + vector_cols]))
            if vector_cols < LIST_COLS:
                nc.scalar.activation(picked[:, 16 * vector_cols:J_PASS], tab[:].indirect(lst[:, c0 + vector_cols:c0 + LIST_COLS]), COPY, scale=sign)
            return picked

        def neg_mean(picked, name):
            sums = keep.tile([P, J_PASS // SET], F32, name=name + "_sums")
            nc.vector.tensor_reduce(sums[:], picked[:].rearrange("p (c r) -> p c r", r=SET), mybir.AxisListType.X, ALU.add)
            twice = keep.tile([P, J_PASS // SET, 2], F32, name=name + "_twice")
            nc.vector.tensor_scalar(twice[:], sums[:].unsqueeze(2).to_broadcast([P, J_PASS // SET, 2]), -1.0 / SET, 0.0, ALU.mult, ALU.add)
            return twice

        def turn_open(picked):
            bank = turn_psum.tile([P, PACK, P], F32, name="bank")
            for t in range(PACK):
                nc.tensor.matmul(bank[:, t, :], picked[:, t:J_PASS:PACK], ident[:], start=(t == 0), stop=False, is_transpose=True)
            return bank

        def turn_close(bank, twice):
            for t in range(PACK):
                nc.tensor.matmul(bank[:, t, :], twice[:].rearrange("p c h -> p (c h)"), ident[:], start=False, stop=(t == PACK - 1), is_transpose=True)

        def centre(picked, name):
            sums = keep.tile([P, J_PASS // SET], F32, name=name + "_sums")
            nc.vector.tensor_reduce(sums[:], picked[:].rearrange("p (c r) -> p c r", r=SET), mybir.AxisListType.X, ALU.add)
            dealt = keep.tile([P, PACK, P], F32, name=name + "_dealt")
            nc.vector.scalar_tensor_tensor(
                out=dealt[:].rearrange("p t q -> p q t"),
                in0=sums[:].unsqueeze(2).to_broadcast([P, J_PASS // SET, SET]),
                scalar=-1.0 / SET,
                in1=picked[:].rearrange("p (c r) -> p c r", r=SET),
                op0=ALU.mult,
                op1=ALU.add,
            )
            return dealt

        def offset(picked, own, name):
            dealt = keep.tile([P, PACK, P], F32, name=name + "_dealt")
            nc.vector.tensor_tensor(
                out=dealt[:].rearrange("p t q -> p q t"),
                in0=picked[:].rearrange("p (q t) -> p q t", t=PACK),
                in1=own.rearrange("p (q t) -> p q t", t=PACK),
                op=ALU.subtract,
            )
            return dealt

        def turn(dealt):
            bank = turn_psum.tile([P, PACK, P], F32, name="bank")
            for t in range(PACK):
                nc.tensor.transpose(bank[:, t, :], dealt[:, t, :], ident[:])
            return bank

        def turn_sum(first, second):
            bank = turn_psum.tile([P, PACK, P], F32, name="bank")
            for s, src in enumerate((first, second)):
                for t in range(PACK):
                    nc.tensor.matmul(bank[:, t, :], src[:, t:J_PASS:PACK], ident[:], start=(s == 0 and t == 0), stop=(s == 1 and t == PACK - 1), is_transpose=True)
            return bank

        def weigh_negated(bank, weight, grouped):
            nc.vector.scalar_tensor_tensor(
                out=grouped,
                in0=bank[:].rearrange("p t c -> p c t"),
                scalar=-1.0,
                in1=weight.unsqueeze(1).to_broadcast([P, P, PACK]),
                op0=ALU.mult,
                op1=ALU.mult,
            )

        def weigh(bank, weight, grouped):
            nc.vector.tensor_tensor(
                out=grouped,
                in0=bank[:].rearrange("p t c -> p c t"),
                in1=weight.unsqueeze(1).to_broadcast([P, P, PACK]),
                op=ALU.mult,
            )

        def quantise(grouped, width, name):
            codes = keep.tile([P, width], U32, name=name + "_codes", tag="last" if name == "u1_1" else name + "_codes", align_bytes=64)
            scales = keep.tile([P, width], U8, name=name + "_scales", align_bytes=64)
            nc.vector.quantize_mx(out=codes[:].bitcast(E5M2X4), scales=scales[:], in_=grouped[:].rearrange("p c t -> p (c t)"))
            return codes, scales

        def product(u_q, g_q):
            acc = acc_psum.tile([P, N], F32, name="acc")
            for a in range(PASSES):
                nc.tensor.matmul_mx(
                    out=acc[:],
                    lhsT=u_q[a][0][:].bitcast(E5M2X4),
                    lhsT_scale=u_q[a][1][:],
                    rhs=g_q[a][0][:].bitcast(E5M2X4),
                    rhs_scale=g_q[a][1][:],
                    start=(a == 0),
                    stop=(a == PASSES - 1),
                )
            return acc

        def place(acc, i):
            w_sb = keep.tile([P, N], F32, name="w_sb%d" % i, tag="xp1_0" if i == 0 else "w_sb1")
            if i == 0:
                nc.scalar.copy(w_sb[:], acc[:])
            else:
                nc.vector.tensor_copy(w_sb[:], acc[:])
            nc.scalar.activation(page[i][:].indirect(w_list[:]), w_sb[:], COPY)

        def finish(i, cuts):
            for h in range(len(cuts) - 1):
                cols = slice(cuts[h], cuts[h + 1])
                res = keep.tile([P, cuts[h + 1] - cuts[h]], F32, name="res%d_%d" % (i, h), tag="last" if (i, h) == (0, 0) else "res%d_%d" % (i, h), align_bytes=64)
                nc.vector.scalar_tensor_tensor(
                    out=res[:], in0=page[i][:, cols], scalar=0.04, in1=old_sb[i][:, cols], op0=ALU.mult, op1=ALU.add
                )
                nc.sync.dma_start(out[rows(i), cols], res[:])

        g_grouped = [
            [keep.tile([P, P, PACK], BF16, name="g_grouped%d_%d" % (i, a), align_bytes=64) for a in range(PASSES)]
            for i in range(2)
        ]
        g_q = [
            (keep.tile([P, N], U32, name="g_codes%d" % a, align_bytes=64), keep.tile([P, N], U8, name="g_scales%d" % a, align_bytes=64))
            for a in range(PASSES)
        ]

        def g_quantise(i, a):
            nc.vector.quantize_mx(out=g_q[a][0][:, rows(i)].bitcast(E5M2X4), scales=g_q[a][1][:, rows(i)], in_=g_grouped[i][a][:].rearrange("p c t -> p (c t)"))
        u_grouped = [
            [keep.tile([P, P, PACK], BF16, name="u_grouped%d_%d" % (i, a), align_bytes=64) for a in range(PASSES)]
            for i in range(2)
        ]
        own = [[own0[:, slots(a)] for a in range(PASSES)], [own1[a][:] for a in range(PASSES)]]

        gp = [[gather(g_tab[i], g_list, a, 16 if (i, a) == (0, 0) else 0, "gp%d_%d" % (i, a)) for a in range(PASSES)] for i in range(2)]
        xp = [[gather(x_tab[i], x_list, a, 0, "xp%d_%d" % (i, a), -1.0 if (i, a) == (1, 0) else 1.0) for a in range(PASSES)] for i in range(2)]

        def g_turn(i, a):
            twice = neg_mean(gp[i][a], "g%d_%d" % (i, a))
            bank = turn_open(gp[i][a])
            turn_close(bank, twice)
            return bank

        def g_weigh(bank, i, a):
            weigh(bank, rb_sb[:, a, 0:PACK], g_grouped[i][a][:])

        def u_turn(i, a):
            return turn(offset(xp[i][a], own[i][a], "u%d_%d" % (i, a)))

        def u_weigh(bank, i, a):
            weigh(bank, ra_sb[:, a, 0:PACK], u_grouped[i][a][:])

        def u_quantise(i, a):
            return quantise(u_grouped[i][a], P, "u%d_%d" % (i, a))

        b00 = g_turn(0, 0)
        b01 = g_turn(0, 1)
        b10 = g_turn(1, 0)
        g_weigh(b00, 0, 0)
        b11 = g_turn(1, 1)
        g_weigh(b01, 0, 1)
        g_quantise(0, 0)
        c00 = u_turn(0, 0)
        g_quantise(0, 1)
        c01 = u_turn(0, 1)
        g_weigh(b10, 1, 0)
        g_weigh(b11, 1, 1)
        g_quantise(1, 0)
        u_weigh(c00, 0, 0)
        g_quantise(1, 1)
        u_weigh(c01, 0, 1)
        q00 = u_quantise(0, 0)
        c10 = turn_sum(own[1][0], xp[1][0][:])
        q01 = u_quantise(0, 1)
        place(product([q00, q01], g_q), 0)
        c11 = u_turn(1, 1)
        weigh_negated(c10, ra_sb[:, 0, 0:PACK], u_grouped[1][0][:])
        q10 = u_quantise(1, 0)
        u_weigh(c11, 1, 1)
        q11 = u_quantise(1, 1)
        place(product([q10, q11], g_q), 1)
        finish(0, [0, 1024])
        finish(1, [0, 256, 512, 768, 1024])
